import numpy as np
import ml_dtypes


def mxq(x, axis, fmt="e4m3"):
    dtype, down = {"e4m3": (ml_dtypes.float8_e4m3fn, 7), "e5m2": (ml_dtypes.float8_e5m2, 14)}[fmt]
    v = np.moveaxis(np.asarray(x, np.float32).astype(ml_dtypes.bfloat16).astype(np.float64), axis, -1)
    blocks = v.reshape(v.shape[:-1] + (-1, 32))
    amax = np.abs(blocks).max(-1, keepdims=True)
    byte = np.maximum(np.where(amax > 0, np.frexp(amax)[1] - 1 + 127, 0) - down, 1)
    scale = np.exp2(byte - 127.0)
    codes = (blocks / scale).astype(np.float32).astype(dtype).astype(np.float64)
    return np.moveaxis((codes * scale).reshape(v.shape), -1, axis)


WIDE = False


def mx_kscale(k):
    if not WIDE:
        return np.ones(k)
    levels = np.array([10, -10, 5, -5, 0])
    if k % 512:
        return np.exp2(np.random.permutation(np.resize(levels, k // 32))).repeat(32)
    a = np.empty((k // 512, 16))
    for p in range(k // 512):
        a[p, :8] = np.random.permutation(np.resize(levels, 8))
        for g in range(8):
            far = levels[np.abs(levels - a[p, g]) >= 10]
            a[p, g + 8] = far[np.random.randint(len(far))]
    return np.exp2(a.ravel()).repeat(32)


def f64(x):
    return np.asarray(x).astype(np.float64)


def striped(idx):
    return np.tile(np.asarray(idx).reshape(-1, 16).T, (8, 1)).astype(np.uint16)


def unstriped(offs):
    return offs[:16].T.reshape(-1).astype(np.int64)


E2M1 = np.array([0.0, 0.5, 1.0, 1.5, 2.0, 3.0, 4.0, 6.0, -0.0, -0.5, -1.0, -1.5, -2.0, -3.0, -4.0, -6.0])


def pack_weight(w, fmt):
    k, n = w.shape
    w = f64(np.asarray(w, np.float32).astype(ml_dtypes.bfloat16)).reshape(k // 32, 32, n)
    amax = np.abs(w).max(1)
    if fmt == "e4m3":
        byte = np.frexp(amax)[1] - 1 + 127 - 7
    else:
        mant, ex = np.frexp(amax / 6.0)
        byte = np.where(mant > 0.5, ex, ex - 1) + 127
    byte = np.clip(np.where(amax > 0, byte, 1), 1, 254)
    scaled = (w * np.exp2(127.0 - byte)[:, None, :]).reshape(k, n).astype(np.float32)
    by_word = np.ascontiguousarray(scaled.reshape(k // 512, 128, 4, n).transpose(0, 1, 3, 2))
    if fmt == "e4m3":
        words = by_word.astype(ml_dtypes.float8_e4m3fn).view(np.uint8)
    else:
        c = by_word.astype(ml_dtypes.float4_e2m1fn).view(np.uint8) & 0xF
        words = (c[..., 0::2] | (c[..., 1::2] << 4)).reshape(k // 512, 128, 2 * n)
    return np.ascontiguousarray(words), np.ascontiguousarray(byte.astype(np.uint8).reshape(k // 512, 16, n))


def unpack_weight(words, scales, fmt):
    g, _, n = scales.shape
    words = np.ascontiguousarray(words).reshape(g, 128, n, -1)
    if fmt == "e4m3":
        vals = words.view(ml_dtypes.float8_e4m3fn).astype(np.float64)
    else:
        nib = np.empty((g, 128, n, 4), np.uint8)
        nib[..., 0::2] = words & 0xF
        nib[..., 1::2] = words >> 4
        vals = E2M1[nib]
    vals = vals * np.repeat(np.exp2(scales.astype(np.float64) - 127.0), 8, axis=1)[..., None]
    return vals.transpose(0, 1, 3, 2).reshape(g * 512, n)


def bf(x):
    return np.asarray(x, np.float32).astype(ml_dtypes.bfloat16)


def planes(Y):
    r, m = Y.shape
    b = f64(bf(Y)).reshape(r // 32, 32, m)
    amax = np.abs(b).max(1)
    byte = np.clip(np.where(amax > 0, np.frexp(amax)[1] - 1 + 127 - 7, 1), 1, 254)
    codes = (b * np.exp2(127.0 - byte)[:, None, :]).reshape(r, m).astype(np.float32).astype(ml_dtypes.float8_e4m3fn).view(np.uint8)
    words = codes.reshape(r // 512, 128, 4, m).transpose(0, 1, 3, 2)
    return np.ascontiguousarray(words), np.ascontiguousarray(byte.astype(np.uint8).reshape(r // 512, 16, m))


D, T, I, Q, E, J = 512, 2048, 512, 256, 512, 512


def setup_inputs():
    n = np.random.standard_normal
    idx = np.random.permutation(T)[:I]
    fd = mx_kscale(D)
    fi = mx_kscale(I)
    fj = mx_kscale(J)
    keysp = pack_weight(n((D, T)) / fd[:, None], "e2m1")
    return {
        "query": (n((D, Q)) * 1.0 / np.sqrt(D) * fd[:, None]).astype(np.float32),
        "keys_words": keysp[0],
        "keys_scales": keysp[1],
        "inv": (n((I, J)) * 1 / np.sqrt(I) * fi[:, None] / fj).astype(np.float32),
        "gain": (np.random.uniform(8.0, 24.0, (1, I)) / fi).astype(np.float32),
        "read": (n((J, E)) * fj[:, None]).astype(np.float32),
        "res": (n((E, Q)) * 4.0).astype(np.float32),
        "offs": striped(idx),
    }


def reference(query, keys_words, keys_scales, inv, gain, read, res, offs):
    idx = unstriped(offs)
    keysu = unpack_weight(keys_words, keys_scales, "e2m1")
    queryq = mxq(f64(query), 0, "e4m3")
    keysidxg = keysu[:, idx]
    a = queryq.T @ keysidxg
    p = np.exp(a - np.max(a, axis=1, keepdims=True))
    f = p / np.sum(p, axis=1, keepdims=True) * f64(gain)
    ft = f.T
    invq = mxq(f64(inv), 0, "e4m3")
    ftq = mxq(ft, 0, "e4m3")
    g = invq.T @ ftq
    readq = mxq(f64(read), 0, "e4m3")
    gq = mxq(g, 0, "e4m3")
    b = readq.T @ gq
    y = b + f64(res)
    words, scales = planes(y)
    return y, words, scales

@@ -1,0 +1,203 @@
+from contextlib import ExitStack
+
+import concourse.mybir as mybir
+from concourse.masks import make_identity
+
+D, T, I, Q, E, J = 512, 2048, 512, 256, 512, 512
+FLOPS = 2 * D * Q * I + 2 * I * J * Q + 2 * J * E * Q
+
+F32 = mybir.dt.float32
+BF16 = mybir.dt.bfloat16
+I32 = mybir.dt.int32
+U32 = mybir.dt.uint32
+U16 = mybir.dt.uint16
+U8 = mybir.dt.uint8
+FP8X4 = mybir.dt.float8_e4m3fn_x4
+FP4X4 = mybir.dt.float4_e2m1fn_x4
+ACT = mybir.ActivationFunctionType
+ALU = mybir.AluOpType
+
+P = 128
+PACK = 4
+HALVES = Q // P
+ALIGN = 64
+
+
+def tile_attend_nystrom_pl_kernel(tc, query, keys_words, keys_scales, inv, gain, read, res, offs, out_0, out_1, out_2):
+    nc = tc.nc
+
+    with ExitStack() as ctx:
+        sb = ctx.enter_context(tc.tile_pool(name="sb", bufs=1))
+        ps = ctx.enter_context(tc.psum_pool(name="ps", bufs=1))
+
+        def sbuf(name, shape, dtype, tag=None):
+            return sb.tile(shape, dtype, name=name, tag=tag or name, align_bytes=ALIGN)
+
+        def bank(name, shape, tag=None):
+            return ps.tile(shape, F32, name=name, tag=tag or name)
+
+        def quantize(name, src, width):
+            codes = sbuf(name + "_codes", [P, width], U32)
+            scales = sbuf(name + "_scales", [P, width], U8)
+            nc.vector.quantize_mx(out=codes[:].bitcast(FP8X4), scales=scales[:], in_=src)
+            return codes, scales
+
+        def weave(copy, dst, src):
+            copy(
+                out=dst.rearrange("p (c i) t -> p c t i", i=4),
+                in_=src.rearrange("p t (c i) -> p c t i", i=4),
+            )
+
+        def deal(copy, dst, src, m0, m1, first=0):
+            copy(
+                out=dst[:].rearrange("p (s m r) -> p m r s", s=PACK, r=PACK)[:, m0:m1],
+                in_=src[:].rearrange("p r (m s) -> p m r s", s=PACK)[:, m0 - first : m1 - first],
+            )
+
+        offsets = sbuf("offsets", [P, I // 16], U16)
+        nc.sync.dma_start(offsets[:], offs)
+
+        pool_scales = sbuf("pool_scales", [P, T], U8)
+        nc.vector.memset(pool_scales[:].bitcast(I32), 0)
+
+        pool_words = sbuf("pool_words", [P, T], U16, tag="words_then_read")
+        nc.sync.dma_start(out=pool_words[:].bitcast(I32), in_=keys_words[0].bitcast(I32))
+        for quad in range(4):
+            nc.sync.dma_start(
+                out=pool_scales[32 * quad : 32 * quad + 4, :].bitcast(I32),
+                in_=keys_scales[0, 4 * quad : 4 * quad + 4, :].bitcast(I32),
+            )
+        query_raw = sbuf("query_raw", [P, PACK, Q], F32, tag="query_then_res")
+        nc.sync.dma_start(out=query_raw[:], in_=query.rearrange("(p t) q -> p t q", t=PACK))
+        inv_raw = []
+        for part in range(2):
+            raw = sbuf("inv_raw%d" % part, [P, PACK, J // 2], F32)
+            cols = slice(part * J // 2, (part + 1) * J // 2)
+            nc.sync.dma_start(out=raw[:], in_=inv.rearrange("(p t) j -> p t j", t=PACK)[:, :, cols])
+            inv_raw.append(raw)
+
+        ident = sbuf("ident", [P, P], F32)
+        make_identity(nc, ident[:])
+        warm = sbuf("warm", [P, 1], F32)
+        nc.scalar.activation(warm[:], ident[:, 0:1], ACT.Exp)
+
+
+        key_scales = sbuf("key_scales", [P, I], U8)
+        nc.vector.tensor_copy(key_scales[:], pool_scales[:].indirect(offsets[:]))
+        gain_cols = sbuf("gain_cols", [P, PACK], F32)
+        nc.scalar.dma_start(out=gain_cols[:], in_=gain.rearrange("o (p t) -> p (o t)", t=PACK))
+        key_words = sbuf("key_words", [P, I], U16)
+        nc.vector.tensor_copy(key_words[:], pool_words[:].indirect(offsets[:]))
+
+        scores = []
+        for h in range(HALVES):
+            query_bf = sbuf("query_bf%d" % h, [P, P, PACK], BF16)
+            weave(nc.scalar.copy, query_bf[:], query_raw[:, :, h * P : (h + 1) * P])
+            codes, scales = quantize("query%d" % h, query_bf[:].rearrange("p q t -> p (q t)"), P)
+            acc = bank("scores%d" % h, [P, I], tag="scores_then_b%d" % h)
+            nc.tensor.matmul_mx(
+                out=acc[:], lhsT=codes[:].bitcast(FP8X4), lhsT_scale=scales[:],
+                rhs=key_words[:].bitcast(FP4X4), rhs_scale=key_scales[:], start=True, stop=True,
+            )
+            scores.append(acc)
+
+        read_raw = sbuf("read_raw", [P, PACK, E], F32, tag="words_then_read")
+        nc.sync.dma_start(out=read_raw[:], in_=read.rearrange("(p t) e -> p t e", t=PACK))
+        res_raw = sbuf("res_raw", [P, PACK, Q], F32, tag="query_then_res")
+        nc.sync.dma_start(out=res_raw[:], in_=res.rearrange("(p t) q -> p t q", t=PACK))
+
+        gain_rows = bank("gain_rows", [P, PACK, P])
+        for t in range(PACK):
+            nc.tensor.transpose(gain_rows[:, t, :], gain_cols[:, t : t + 1].to_broadcast([P, P]), ident[:])
+
+        probs, sums = [], []
+        for h in range(HALVES):
+            neg_max = sbuf("neg_max%d" % h, [P, 1], F32)
+            nc.vector.tensor_reduce(neg_max[:], scores[h][:], mybir.AxisListType.X, ALU.max, negate=True)
+            prob = sbuf("prob%d" % h, [P, 2, P, 2], F32)
+            row_sum = sbuf("row_sum%d" % h, [P, 1], F32)
+            nc.scalar.activation(
+                prob[:], scores[h][:].rearrange("q (p u e) -> q u p e", u=2, e=2), ACT.Exp,
+                bias=neg_max[:], scale=1.0, accum_out=row_sum[:],
+            )
+            probs.append(prob)
+            sums.append(row_sum)
+
+        ft_q = []
+        for h in range(HALVES):
+            recip = sbuf("recip%d" % h, [P, 1], F32)
+            nc.vector.reciprocal(recip[:], sums[h][:])
+            turned = bank("turned%d" % h, [P, 2, P])
+            for u in range(2):
+                f_bf = sbuf("f_bf%d%d" % (h, u), [P, P, 2], BF16)
+                nc.vector.scalar_tensor_tensor(
+                    f_bf[:], probs[h][:, u], recip[:],
+                    gain_rows[:, 2 * u : 2 * u + 2, :].rearrange("q e p -> q p e"), ALU.mult, ALU.mult,
+                )
+                nc.tensor.transpose(turned[:, u, :], f_bf[:].rearrange("q p e -> q (p e)").bitcast(F32), ident[:])
+            ft_bf = sbuf("ft_bf%d" % h, [P, P * PACK], BF16)
+            nc.scalar.copy(
+                out=ft_bf[:].bitcast(F32).rearrange("p (q u) -> p q u", u=2),
+                in_=turned[:].rearrange("p u q -> p q u"),
+            )
+            ft_q.append(quantize("ft%d" % h, ft_bf[:], P))
+
+        inv_bf = sbuf("inv_bf", [P, J * PACK], BF16)
+        deal(nc.vector.tensor_copy, inv_bf, inv_raw[0], 0, 32, 0)
+        deal(nc.scalar.copy, inv_bf, inv_raw[0], 32, 64, 0)
+        deal(nc.scalar.copy, inv_bf, inv_raw[1], 64, 80, 64)
+        deal(nc.scalar.copy, inv_bf, inv_raw[1], 80, 96, 64)
+        deal(nc.scalar.copy, inv_bf, inv_raw[1], 96, 112, 64)
+        deal(nc.vector.tensor_copy, inv_bf, inv_raw[1], 112, 128, 64)
+        inv_codes, inv_scales = quantize("inv", inv_bf[:], J)
+
+        def product(acc, w_codes, w_scales, x_codes, x_scales):
+            for s in range(PACK):
+                cols = slice(s * P, (s + 1) * P)
+                nc.tensor.matmul_mx(
+                    out=acc[:, s, :], lhsT=w_codes[:, cols].bitcast(FP8X4), lhsT_scale=w_scales[:, cols],
+                    rhs=x_codes[:].bitcast(FP8X4), rhs_scale=x_scales[:], start=True, stop=True,
+                )
+
+        g_q = []
+        for h in range(HALVES):
+            g_acc = bank("g%d" % h, [P, PACK, P])
+            product(g_acc, inv_codes, inv_scales, *ft_q[h])
+            g_bf = sbuf("g_bf%d" % h, [P, P, PACK], BF16)
+            nc.scalar.copy(out=g_bf[:], in_=g_acc[:].rearrange("p t q -> p q t"))
+            g_q.append(quantize("g%d" % h, g_bf[:].rearrange("p q t -> p (q t)"), P))
+
+        read_bf = sbuf("read_bf", [P, E * PACK], BF16)
+        deal(nc.scalar.copy, read_bf, read_raw, 0, 16)
+        deal(nc.scalar.copy, read_bf, read_raw, 16, 32)
+        deal(nc.scalar.copy, read_bf, read_raw, 32, 48)
+        deal(nc.scalar.copy, read_bf, read_raw, 48, 64)
+        deal(nc.vector.tensor_copy, read_bf, read_raw, 64, 96)
+        deal(nc.vector.tensor_copy, read_bf, read_raw, 96, 128)
+        read_codes, read_scales = quantize("read", read_bf[:], E)
+
+        y_codes = sbuf("y_codes", [P, Q], U32)
+        y_scales = sbuf("y_scales", [P, Q], U8)
+        out_rows = out_0.rearrange("(p t) q -> p t q", t=PACK)
+        out_words = out_1[0].rearrange("p c r -> p (c r)").bitcast(I32)
+        for h in range(HALVES):
+            cols = slice(h * P, (h + 1) * P)
+            b_acc = bank("b%d" % h, [P, PACK, P], tag="scores_then_b%d" % h)
+            product(b_acc, read_codes, read_scales, *g_q[h])
+            y = sbuf("y%d" % h, [P, PACK, P], F32)
+            nc.vector.tensor_tensor(y[:], b_acc[:], res_raw[:, :, cols], ALU.add)
+            nc.sync.dma_start(out=out_rows[:, :, cols], in_=y[:])
+            y_bf = sbuf("y_bf%d" % h, [P, P, PACK], BF16)
+            copy = nc.scalar.copy if h == 0 else nc.vector.tensor_copy
+            weave(copy, y_bf[:], y[:])
+            nc.vector.quantize_mx(
+                out=y_codes[:, cols].bitcast(FP8X4), scales=y_scales[:, cols],
+                in_=y_bf[:].rearrange("p q t -> p (q t)"),
+            )
+            nc.sync.dma_start(out=out_words[:, cols], in_=y_codes[:, cols].bitcast(I32))
+        for quad in range(4):
+            queue = nc.scalar if quad % 2 == 0 else nc.sync
+            queue.dma_start(
+                out=out_2[0, 4 * quad : 4 * quad + 4, :].bitcast(I32),
+                in_=y_scales[32 * quad : 32 * quad + 4, :].bitcast(I32),
+            )

@@ -36,8 +36,8 @@ def tile_attend_nystrom_pl_kernel(tc, query, keys_words, keys_scales, inv, gain,
         def bank(name, shape, tag=None):
             return ps.tile(shape, F32, name=name, tag=tag or name)
 
-        def quantize(name, src, width):
-            codes = sbuf(name + "_codes", [P, width], U32)
+        def quantize(name, src, width, tag=None):
+            codes = sbuf(name + "_codes", [P, width], U32, tag=tag)
             scales = sbuf(name + "_scales", [P, width], U8)
             nc.vector.quantize_mx(out=codes[:].bitcast(FP8X4), scales=scales[:], in_=src)
             return codes, scales
@@ -48,10 +48,16 @@ def tile_attend_nystrom_pl_kernel(tc, query, keys_words, keys_scales, inv, gain,
                 in_=src.rearrange("p t (c i) -> p c t i", i=4),
             )
 
-        def deal(copy, dst, src, m0, m1, first=0):
+        def deal(copy, dst, src, pair, m0, m1, first=0):
             copy(
-                out=dst[:].rearrange("p (s m r) -> p m r s", s=PACK, r=PACK)[:, m0:m1],
-                in_=src[:].rearrange("p r (m s) -> p m r s", s=PACK)[:, m0 - first : m1 - first],
+                out=dst[:].rearrange("p (s m r) -> p m r s", s=2, r=PACK)[:, m0:m1],
+                in_=src[:].rearrange("p r (m s) -> p m r s", s=PACK)[:, m0 - first : m1 - first, :, 2 * pair : 2 * pair + 2],
+            )
+
+        def deal_rows(copy, dst, src, pair, m0, m1, first=0):
+            copy(
+                out=dst[:].rearrange("p (s m r) -> p s m r", s=2, r=PACK)[:, :, m0:m1],
+                in_=src[:].rearrange("p r (m s) -> p s m r", s=PACK)[:, 2 * pair : 2 * pair + 2, m0 - first : m1 - first],
             )
 
         offsets = sbuf("offsets", [P, I // 16], U16)
@@ -110,82 +116,95 @@ def tile_attend_nystrom_pl_kernel(tc, query, keys_words, keys_scales, inv, gain,
         for t in range(PACK):
             nc.tensor.transpose(gain_rows[:, t, :], gain_cols[:, t : t + 1].to_broadcast([P, P]), ident[:])
 
+        inv_bf = [sbuf("inv_bf%d" % pair, [P, 2 * J], BF16) for pair in range(2)]
+        for pair in range(2):
+            deal(nc.scalar.copy, inv_bf[pair], inv_raw[0], pair, 0, 64)
         probs, sums = [], []
         for h in range(HALVES):
-            neg_max = sbuf("neg_max%d" % h, [P, 1], F32)
-            nc.vector.tensor_reduce(neg_max[:], scores[h][:], mybir.AxisListType.X, ALU.max, negate=True)
+            neg_max = inv_bf[1 - h][:, 2 * J - 2 : 2 * J].bitcast(F32)
+            nc.vector.tensor_reduce(neg_max, scores[h][:], mybir.AxisListType.X, ALU.max, negate=True)
             prob = sbuf("prob%d" % h, [P, 2, P, 2], F32)
             row_sum = sbuf("row_sum%d" % h, [P, 1], F32)
             nc.scalar.activation(
                 prob[:], scores[h][:].rearrange("q (p u e) -> q u p e", u=2, e=2), ACT.Exp,
-                bias=neg_max[:], scale=1.0, accum_out=row_sum[:],
+                bias=neg_max, scale=1.0, accum_out=row_sum[:],
             )
             probs.append(prob)
             sums.append(row_sum)
 
+        recips = [sbuf("recip%d" % h, [P, 1], F32) for h in range(HALVES)]
+        turned = [bank("turned%d" % h, [P, 2, P]) for h in range(HALVES)]
+
+        def weigh(h, u):
+            f_bf = sbuf("f_bf%d%d" % (h, u), [P, P, 2], BF16)
+            nc.vector.scalar_tensor_tensor(
+                f_bf[:], probs[h][:, u], recips[h][:],
+                gain_rows[:, 2 * u : 2 * u + 2, :].rearrange("q e p -> q p e"), ALU.mult, ALU.mult,
+            )
+            nc.tensor.transpose(turned[h][:, u, :], f_bf[:].rearrange("q p e -> q (p e)").bitcast(F32), ident[:])
+
+        nc.vector.reciprocal(recips[0][:], sums[0][:])
+        weigh(0, 0)
+        nc.vector.reciprocal(recips[1][:], sums[1][:])
+        weigh(0, 1)
+        weigh(1, 0)
+        weigh(1, 1)
         ft_q = []
         for h in range(HALVES):
-            recip = sbuf("recip%d" % h, [P, 1], F32)
-            nc.vector.reciprocal(recip[:], sums[h][:])
-            turned = bank("turned%d" % h, [P, 2, P])
-            for u in range(2):
-                f_bf = sbuf("f_bf%d%d" % (h, u), [P, P, 2], BF16)
-                nc.vector.scalar_tensor_tensor(
-                    f_bf[:], probs[h][:, u], recip[:],
-                    gain_rows[:, 2 * u : 2 * u + 2, :].rearrange("q e p -> q p e"), ALU.mult, ALU.mult,
-                )
-                nc.tensor.transpose(turned[:, u, :], f_bf[:].rearrange("q p e -> q (p e)").bitcast(F32), ident[:])
             ft_bf = sbuf("ft_bf%d" % h, [P, P * PACK], BF16)
             nc.scalar.copy(
                 out=ft_bf[:].bitcast(F32).rearrange("p (q u) -> p q u", u=2),
-                in_=turned[:].rearrange("p u q -> p q u"),
+                in_=turned[h][:].rearrange("p u q -> p q u"),
             )
             ft_q.append(quantize("ft%d" % h, ft_bf[:], P))
 
-        inv_bf = sbuf("inv_bf", [P, J * PACK], BF16)
-        deal(nc.vector.tensor_copy, inv_bf, inv_raw[0], 0, 32, 0)
-        deal(nc.scalar.copy, inv_bf, inv_raw[0], 32, 64, 0)
-        deal(nc.scalar.copy, inv_bf, inv_raw[1], 64, 80, 64)
-        deal(nc.scalar.copy, inv_bf, inv_raw[1], 80, 96, 64)
-        deal(nc.scalar.copy, inv_bf, inv_raw[1], 96, 112, 64)
-        deal(nc.vector.tensor_copy, inv_bf, inv_raw[1], 112, 128, 64)
-        inv_codes, inv_scales = quantize("inv", inv_bf[:], J)
+        deal(nc.scalar.copy, inv_bf[1], inv_raw[1], 1, 64, 128, 64)
+        deal(nc.scalar.copy, inv_bf[0], inv_raw[1], 0, 64, 128, 64)
+        inv_q = [None, None]
+        inv_q[1] = quantize("inv1", inv_bf[1][:], J // 2, tag="recip0")
+        inv_q[0] = quantize("inv0", inv_bf[0][:], J // 2)
 
-        def product(acc, w_codes, w_scales, x_codes, x_scales):
+        def product(accs, weights, x_codes, x_scales):
             for s in range(PACK):
-                cols = slice(s * P, (s + 1) * P)
+                w_codes, w_scales = weights[s // 2]
+                cols = slice(s % 2 * P, (s % 2 + 1) * P)
                 nc.tensor.matmul_mx(
-                    out=acc[:, s, :], lhsT=w_codes[:, cols].bitcast(FP8X4), lhsT_scale=w_scales[:, cols],
+                    out=accs[s], lhsT=w_codes[:, cols].bitcast(FP8X4), lhsT_scale=w_scales[:, cols],
                     rhs=x_codes[:].bitcast(FP8X4), rhs_scale=x_scales[:], start=True, stop=True,
                 )
+
+        read_bf = [
+            sbuf("read_bf0", [P, 2 * E], BF16, tag="f_bf11"),
+            sbuf("read_bf1", [P, 2 * E], BF16, tag="ft_bf1"),
+        ]
+        for m0 in (0, 32, 64):
+            deal(nc.scalar.copy, read_bf[0], read_raw, 0, m0, m0 + 32)
+        deal(nc.vector.tensor_copy, read_bf[0], read_raw, 0, 96, 128)
+        deal(nc.vector.tensor_copy, read_bf[1], read_raw, 1, 0, 128)
 
         g_q = []
         for h in range(HALVES):
             g_acc = bank("g%d" % h, [P, PACK, P])
-            product(g_acc, inv_codes, inv_scales, *ft_q[h])
+            product([g_acc[:, s, :] for s in range(PACK)], inv_q, *ft_q[h])
             g_bf = sbuf("g_bf%d" % h, [P, P, PACK], BF16)
             nc.scalar.copy(out=g_bf[:], in_=g_acc[:].rearrange("p t q -> p q t"))
             g_q.append(quantize("g%d" % h, g_bf[:].rearrange("p q t -> p (q t)"), P))
 
-        read_bf = sbuf("read_bf", [P, E * PACK], BF16)
-        deal(nc.scalar.copy, read_bf, read_raw, 0, 16)
-        deal(nc.scalar.copy, read_bf, read_raw, 16, 32)
-        deal(nc.scalar.copy, read_bf, read_raw, 32, 48)
-        deal(nc.scalar.copy, read_bf, read_raw, 48, 64)
-        deal(nc.vector.tensor_copy, read_bf, read_raw, 64, 96)
-        deal(nc.vector.tensor_copy, read_bf, read_raw, 96, 128)
-        read_codes, read_scales = quantize("read", read_bf[:], E)
+        read_q = [quantize("read%d" % pair, read_bf[pair][:], E // 2) for pair in range(2)]
 
+        b_tags = (("scores_then_b0", "scores_then_b1"), ("turned0", "turned1"))
         y_codes = sbuf("y_codes", [P, Q], U32)
         y_scales = sbuf("y_scales", [P, Q], U8)
         out_rows = out_0.rearrange("(p t) q -> p t q", t=PACK)
         out_words = out_1[0].rearrange("p c r -> p (c r)").bitcast(I32)
         for h in range(HALVES):
             cols = slice(h * P, (h + 1) * P)
-            b_acc = bank("b%d" % h, [P, PACK, P], tag="scores_then_b%d" % h)
-            product(b_acc, read_codes, read_scales, *g_q[h])
+            b_acc = [bank("b%d%d" % (h, pair), [P, 2, P], tag=b_tags[h][pair]) for pair in range(2)]
+            product([b_acc[s // 2][:, s % 2, :] for s in range(PACK)], read_q, *g_q[h])
             y = sbuf("y%d" % h, [P, PACK, P], F32)
-            nc.vector.tensor_tensor(y[:], b_acc[:], res_raw[:, :, cols], ALU.add)
+            for pair in range(2):
+                planes = slice(2 * pair, 2 * pair + 2)
+                nc.vector.tensor_tensor(y[:, planes, :], b_acc[pair][:], res_raw[:, planes, cols], ALU.add)
             nc.sync.dma_start(out=out_rows[:, :, cols], in_=y[:])
             y_bf = sbuf("y_bf%d" % h, [P, P, PACK], BF16)
             copy = nc.scalar.copy if h == 0 else nc.vector.tensor_copy

@@ -117,11 +117,14 @@ def tile_attend_nystrom_pl_kernel(tc, query, keys_words, keys_scales, inv, gain,
             nc.tensor.transpose(gain_rows[:, t, :], gain_cols[:, t : t + 1].to_broadcast([P, P]), ident[:])
 
         inv_bf = [sbuf("inv_bf%d" % pair, [P, 2 * J], BF16) for pair in range(2)]
-        for pair in range(2):
-            deal(nc.scalar.copy, inv_bf[pair], inv_raw[0], pair, 0, 64)
+        deal(nc.scalar.copy, inv_bf[0], inv_raw[0], 0, 0, 64)
+        deal_rows(nc.gpsimd.tensor_copy, inv_bf[1], inv_raw[0], 1, 0, 64)
+        deal_rows(nc.gpsimd.tensor_copy, inv_bf[1], inv_raw[1], 1, 64, 128, 64)
+        neg_max0 = sbuf("neg_max0", [P, 1], F32)
+        neg_maxes = [neg_max0[:], inv_bf[0][:, 2 * J - 2 : 2 * J].bitcast(F32)]
         probs, sums = [], []
         for h in range(HALVES):
-            neg_max = inv_bf[1 - h][:, 2 * J - 2 : 2 * J].bitcast(F32)
+            neg_max = neg_maxes[h]
             nc.vector.tensor_reduce(neg_max, scores[h][:], mybir.AxisListType.X, ALU.max, negate=True)
             prob = sbuf("prob%d" % h, [P, 2, P, 2], F32)
             row_sum = sbuf("row_sum%d" % h, [P, 1], F32)
@@ -135,13 +138,17 @@ def tile_attend_nystrom_pl_kernel(tc, query, keys_words, keys_scales, inv, gain,
         recips = [sbuf("recip%d" % h, [P, 1], F32) for h in range(HALVES)]
         turned = [bank("turned%d" % h, [P, 2, P]) for h in range(HALVES)]
 
+        read_bf0 = sbuf("read_bf0", [P, 2 * E], BF16)
+        f_first = [sbuf("f_bf%d0" % h, [P, 2 * P], BF16) for h in range(HALVES)]
+        f_bfs = [[f_first[0][:], read_bf0[:, 512:768]], [f_first[1][:], read_bf0[:, 256:512]]]
+
         def weigh(h, u):
-            f_bf = sbuf("f_bf%d%d" % (h, u), [P, P, 2], BF16)
+            f_bf = f_bfs[h][u]
             nc.vector.scalar_tensor_tensor(
-                f_bf[:], probs[h][:, u], recips[h][:],
+                f_bf.rearrange("q (p e) -> q p e", e=2), probs[h][:, u], recips[h][:],
                 gain_rows[:, 2 * u : 2 * u + 2, :].rearrange("q e p -> q p e"), ALU.mult, ALU.mult,
             )
-            nc.tensor.transpose(turned[h][:, u, :], f_bf[:].rearrange("q p e -> q (p e)").bitcast(F32), ident[:])
+            nc.tensor.transpose(turned[h][:, u, :], f_bf.bitcast(F32), ident[:])
 
         nc.vector.reciprocal(recips[0][:], sums[0][:])
         weigh(0, 0)
@@ -158,10 +165,9 @@ def tile_attend_nystrom_pl_kernel(tc, query, keys_words, keys_scales, inv, gain,
             )
             ft_q.append(quantize("ft%d" % h, ft_bf[:], P))
 
-        deal(nc.scalar.copy, inv_bf[1], inv_raw[1], 1, 64, 128, 64)
         deal(nc.scalar.copy, inv_bf[0], inv_raw[1], 0, 64, 128, 64)
         inv_q = [None, None]
-        inv_q[1] = quantize("inv1", inv_bf[1][:], J // 2, tag="recip0")
+        inv_q[1] = quantize("inv1", inv_bf[1][:], J // 2, tag="recip1")
         inv_q[0] = quantize("inv0", inv_bf[0][:], J // 2)
 
         def product(accs, weights, x_codes, x_scales):
@@ -174,11 +180,11 @@ def tile_attend_nystrom_pl_kernel(tc, query, keys_words, keys_scales, inv, gain,
                 )
 
         read_bf = [
-            sbuf("read_bf0", [P, 2 * E], BF16, tag="f_bf11"),
+            read_bf0,
             sbuf("read_bf1", [P, 2 * E], BF16, tag="ft_bf1"),
         ]
-        for m0 in (0, 32, 64):
-            deal(nc.scalar.copy, read_bf[0], read_raw, 0, m0, m0 + 32)
+        deal(nc.scalar.copy, read_bf[0], read_raw, 0, 0, 32)
+        deal(nc.scalar.copy, read_bf[0], read_raw, 0, 32, 96)
         deal(nc.vector.tensor_copy, read_bf[0], read_raw, 0, 96, 128)
         deal(nc.vector.tensor_copy, read_bf[1], read_raw, 1, 0, 128)
 
@@ -193,6 +199,7 @@ def tile_attend_nystrom_pl_kernel(tc, query, keys_words, keys_scales, inv, gain,
         read_q = [quantize("read%d" % pair, read_bf[pair][:], E // 2) for pair in range(2)]
 
         b_tags = (("scores_then_b0", "scores_then_b1"), ("turned0", "turned1"))
+        y = sbuf("y", [P, PACK, Q], F32)
         y_codes = sbuf("y_codes", [P, Q], U32)
         y_scales = sbuf("y_scales", [P, Q], U8)
         out_rows = out_0.rearrange("(p t) q -> p t q", t=PACK)
@@ -201,19 +208,22 @@ def tile_attend_nystrom_pl_kernel(tc, query, keys_words, keys_scales, inv, gain,
             cols = slice(h * P, (h + 1) * P)
             b_acc = [bank("b%d%d" % (h, pair), [P, 2, P], tag=b_tags[h][pair]) for pair in range(2)]
             product([b_acc[s // 2][:, s % 2, :] for s in range(PACK)], read_q, *g_q[h])
-            y = sbuf("y%d" % h, [P, PACK, P], F32)
             for pair in range(2):
                 planes = slice(2 * pair, 2 * pair + 2)
-                nc.vector.tensor_tensor(y[:, planes, :], b_acc[pair][:], res_raw[:, planes, cols], ALU.add)
-            nc.sync.dma_start(out=out_rows[:, :, cols], in_=y[:])
+                nc.vector.tensor_tensor(y[:, planes, cols], b_acc[pair][:], res_raw[:, planes, cols], ALU.add)
+                if h == HALVES - 1:
+                    nc.sync.dma_start(out=out_rows[:, planes, :], in_=y[:, planes, :])
             y_bf = sbuf("y_bf%d" % h, [P, P, PACK], BF16)
-            copy = nc.scalar.copy if h == 0 else nc.vector.tensor_copy
-            weave(copy, y_bf[:], y[:])
+            if h == 0:
+                weave(nc.scalar.copy, y_bf[:], y[:, :, cols])
+            else:
+                weave(nc.vector.tensor_copy, y_bf[:, :80, :], y[:, :, P : P + 80])
+                weave(nc.scalar.copy, y_bf[:, 80:, :], y[:, :, P + 80 :])
             nc.vector.quantize_mx(
                 out=y_codes[:, cols].bitcast(FP8X4), scales=y_scales[:, cols],
                 in_=y_bf[:].rearrange("p q t -> p (q t)"),
             )
-            nc.sync.dma_start(out=out_words[:, cols], in_=y_codes[:, cols].bitcast(I32))
+            (nc.sync, nc.scalar)[h].dma_start(out=out_words[:, cols], in_=y_codes[:, cols].bitcast(I32))
         for quad in range(4):
             queue = nc.scalar if quad % 2 == 0 else nc.sync
             queue.dma_start(

from contextlib import ExitStack

import concourse.mybir as mybir
from concourse.masks import make_identity

D, T, I, Q, E, J = 512, 2048, 512, 256, 512, 512
FLOPS = 2 * D * Q * I + 2 * I * J * Q + 2 * J * E * Q

F32 = mybir.dt.float32
BF16 = mybir.dt.bfloat16
I32 = mybir.dt.int32
U32 = mybir.dt.uint32
U16 = mybir.dt.uint16
U8 = mybir.dt.uint8
FP8X4 = mybir.dt.float8_e4m3fn_x4
FP4X4 = mybir.dt.float4_e2m1fn_x4
ACT = mybir.ActivationFunctionType
ALU = mybir.AluOpType

P = 128
PACK = 4
HALVES = Q // P
ALIGN = 64


def tile_attend_nystrom_pl_kernel(tc, query, keys_words, keys_scales, inv, gain, read, res, offs, out_0, out_1, out_2):
    nc = tc.nc

    with ExitStack() as ctx:
        sb = ctx.enter_context(tc.tile_pool(name="sb", bufs=1))
        ps = ctx.enter_context(tc.psum_pool(name="ps", bufs=1))

        def sbuf(name, shape, dtype, tag=None):
            return sb.tile(shape, dtype, name=name, tag=tag or name, align_bytes=ALIGN)

        def bank(name, shape, tag=None):
            return ps.tile(shape, F32, name=name, tag=tag or name)

        def quantize(name, src, width, tag=None):
            codes = sbuf(name + "_codes", [P, width], U32, tag=tag)
            scales = sbuf(name + "_scales", [P, width], U8)
            nc.vector.quantize_mx(out=codes[:].bitcast(FP8X4), scales=scales[:], in_=src)
            return codes, scales

        def weave(copy, dst, src):
            copy(
                out=dst.rearrange("p (c i) t -> p c t i", i=4),
                in_=src.rearrange("p t (c i) -> p c t i", i=4),
            )

        def deal(copy, dst, src, pair, m0, m1, first=0):
            copy(
                out=dst[:].rearrange("p (s m r) -> p m r s", s=2, r=PACK)[:, m0:m1],
                in_=src[:].rearrange("p r (m s) -> p m r s", s=PACK)[:, m0 - first : m1 - first, :, 2 * pair : 2 * pair + 2],
            )

        def deal_rows(copy, dst, src, pair, m0, m1, first=0):
            copy(
                out=dst[:].rearrange("p (s m r) -> p s m r", s=2, r=PACK)[:, :, m0:m1],
                in_=src[:].rearrange("p r (m s) -> p s m r", s=PACK)[:, 2 * pair : 2 * pair + 2, m0 - first : m1 - first],
            )

        offsets = sbuf("offsets", [P, I // 16], U16)
        nc.sync.dma_start(offsets[:], offs)

        pool_scales = sbuf("pool_scales", [P, T], U8)
        nc.vector.memset(pool_scales[:].bitcast(I32), 0)

        pool_words = sbuf("pool_words", [P, T], U16, tag="words_then_read")
        nc.sync.dma_start(out=pool_words[:].bitcast(I32), in_=keys_words[0].bitcast(I32))
        for quad in range(4):
            nc.sync.dma_start(
                out=pool_scales[32 * quad : 32 * quad + 4, :].bitcast(I32),
                in_=keys_scales[0, 4 * quad : 4 * quad + 4, :].bitcast(I32),
            )
        query_raw = sbuf("query_raw", [P, PACK, Q], F32, tag="query_then_res")
        nc.sync.dma_start(out=query_raw[:], in_=query.rearrange("(p t) q -> p t q", t=PACK))
        inv_raw = []
        for part in range(2):
            raw = sbuf("inv_raw%d" % part, [P, PACK, J // 2], F32)
            cols = slice(part * J // 2, (part + 1) * J // 2)
            nc.sync.dma_start(out=raw[:], in_=inv.rearrange("(p t) j -> p t j", t=PACK)[:, :, cols])
            inv_raw.append(raw)

        ident = sbuf("ident", [P, P], F32)
        make_identity(nc, ident[:])
        warm = sbuf("warm", [P, 1], F32)
        nc.scalar.activation(warm[:], ident[:, 0:1], ACT.Exp)


        key_scales = sbuf("key_scales", [P, I], U8)
        nc.vector.tensor_copy(key_scales[:], pool_scales[:].indirect(offsets[:]))
        gain_cols = sbuf("gain_cols", [P, PACK], F32)
        nc.scalar.dma_start(out=gain_cols[:], in_=gain.rearrange("o (p t) -> p (o t)", t=PACK))
        key_words = sbuf("key_words", [P, I], U16)
        nc.vector.tensor_copy(key_words[:], pool_words[:].indirect(offsets[:]))

        scores = []
        for h in range(HALVES):
            query_bf = sbuf("query_bf%d" % h, [P, P, PACK], BF16)
            weave(nc.scalar.copy, query_bf[:], query_raw[:, :, h * P : (h + 1) * P])
            codes, scales = quantize("query%d" % h, query_bf[:].rearrange("p q t -> p (q t)"), P)
            acc = bank("scores%d" % h, [P, I], tag="scores_then_b%d" % h)
            nc.tensor.matmul_mx(
                out=acc[:], lhsT=codes[:].bitcast(FP8X4), lhsT_scale=scales[:],
                rhs=key_words[:].bitcast(FP4X4), rhs_scale=key_scales[:], start=True, stop=True,
            )
            scores.append(acc)

        read_raw = sbuf("read_raw", [P, PACK, E], F32, tag="words_then_read")
        nc.sync.dma_start(out=read_raw[:], in_=read.rearrange("(p t) e -> p t e", t=PACK))
        res_raw = sbuf("res_raw", [P, PACK, Q], F32, tag="query_then_res")
        nc.sync.dma_start(out=res_raw[:], in_=res.rearrange("(p t) q -> p t q", t=PACK))

        gain_rows = bank("gain_rows", [P, PACK, P])
        for t in range(PACK):
            nc.tensor.transpose(gain_rows[:, t, :], gain_cols[:, t : t + 1].to_broadcast([P, P]), ident[:])

        inv_bf = [sbuf("inv_bf%d" % pair, [P, 2 * J], BF16) for pair in range(2)]
        deal(nc.scalar.copy, inv_bf[0], inv_raw[0], 0, 0, 64)
        deal_rows(nc.gpsimd.tensor_copy, inv_bf[1], inv_raw[0], 1, 0, 64)
        deal_rows(nc.gpsimd.tensor_copy, inv_bf[1], inv_raw[1], 1, 64, 128, 64)
        neg_max0 = sbuf("neg_max0", [P, 1], F32)
        neg_maxes = [neg_max0[:], inv_bf[0][:, 2 * J - 2 : 2 * J].bitcast(F32)]
        probs, sums = [], []
        for h in range(HALVES):
            neg_max = neg_maxes[h]
            nc.vector.tensor_reduce(neg_max, scores[h][:], mybir.AxisListType.X, ALU.max, negate=True)
            prob = sbuf("prob%d" % h, [P, 2, P, 2], F32)
            row_sum = sbuf("row_sum%d" % h, [P, 1], F32)
            nc.scalar.activation(
                prob[:], scores[h][:].rearrange("q (p u e) -> q u p e", u=2, e=2), ACT.Exp,
                bias=neg_max, scale=1.0, accum_out=row_sum[:],
            )
            probs.append(prob)
            sums.append(row_sum)

        recips = [sbuf("recip%d" % h, [P, 1], F32) for h in range(HALVES)]
        turned = [bank("turned%d" % h, [P, 2, P]) for h in range(HALVES)]

        read_bf0 = sbuf("read_bf0", [P, 2 * E], BF16)
        f_first = [sbuf("f_bf%d0" % h, [P, 2 * P], BF16) for h in range(HALVES)]
        f_bfs = [[f_first[0][:], read_bf0[:, 512:768]], [f_first[1][:], read_bf0[:, 256:512]]]

        def weigh(h, u):
            f_bf = f_bfs[h][u]
            nc.vector.scalar_tensor_tensor(
                f_bf.rearrange("q (p e) -> q p e", e=2), probs[h][:, u], recips[h][:],
                gain_rows[:, 2 * u : 2 * u + 2, :].rearrange("q e p -> q p e"), ALU.mult, ALU.mult,
            )
            nc.tensor.transpose(turned[h][:, u, :], f_bf.bitcast(F32), ident[:])

        nc.vector.reciprocal(recips[0][:], sums[0][:])
        weigh(0, 0)
        nc.vector.reciprocal(recips[1][:], sums[1][:])
        weigh(0, 1)
        weigh(1, 0)
        weigh(1, 1)
        ft_q = []
        for h in range(HALVES):
            ft_bf = sbuf("ft_bf%d" % h, [P, P * PACK], BF16)
            nc.scalar.copy(
                out=ft_bf[:].bitcast(F32).rearrange("p (q u) -> p q u", u=2),
                in_=turned[h][:].rearrange("p u q -> p q u"),
            )
            ft_q.append(quantize("ft%d" % h, ft_bf[:], P))

        deal(nc.scalar.copy, inv_bf[0], inv_raw[1], 0, 64, 128, 64)
        inv_q = [None, None]
        inv_q[1] = quantize("inv1", inv_bf[1][:], J // 2, tag="recip1")
        inv_q[0] = quantize("inv0", inv_bf[0][:], J // 2)

        def product(accs, weights, x_codes, x_scales):
            for s in range(PACK):
                w_codes, w_scales = weights[s // 2]
                cols = slice(s % 2 * P, (s % 2 + 1) * P)
                nc.tensor.matmul_mx(
                    out=accs[s], lhsT=w_codes[:, cols].bitcast(FP8X4), lhsT_scale=w_scales[:, cols],
                    rhs=x_codes[:].bitcast(FP8X4), rhs_scale=x_scales[:], start=True, stop=True,
                )

        read_bf = [
            read_bf0,
            sbuf("read_bf1", [P, 2 * E], BF16, tag="ft_bf1"),
        ]
        deal(nc.scalar.copy, read_bf[0], read_raw, 0, 0, 32)
        deal(nc.scalar.copy, read_bf[0], read_raw, 0, 32, 96)
        deal(nc.vector.tensor_copy, read_bf[0], read_raw, 0, 96, 128)
        deal(nc.vector.tensor_copy, read_bf[1], read_raw, 1, 0, 128)

        g_q = []
        for h in range(HALVES):
            g_acc = bank("g%d" % h, [P, PACK, P])
            product([g_acc[:, s, :] for s in range(PACK)], inv_q, *ft_q[h])
            g_bf = sbuf("g_bf%d" % h, [P, P, PACK], BF16)
            nc.scalar.copy(out=g_bf[:], in_=g_acc[:].rearrange("p t q -> p q t"))
            g_q.append(quantize("g%d" % h, g_bf[:].rearrange("p q t -> p (q t)"), P))

        read_q = [quantize("read%d" % pair, read_bf[pair][:], E // 2) for pair in range(2)]

        b_tags = (("scores_then_b0", "scores_then_b1"), ("turned0", "turned1"))
        y = sbuf("y", [P, PACK, Q], F32)
        y_codes = sbuf("y_codes", [P, Q], U32)
        y_scales = sbuf("y_scales", [P, Q], U8)
        out_rows = out_0.rearrange("(p t) q -> p t q", t=PACK)
        out_words = out_1[0].rearrange("p c r -> p (c r)").bitcast(I32)
        for h in range(HALVES):
            cols = slice(h * P, (h + 1) * P)
            b_acc = [bank("b%d%d" % (h, pair), [P, 2, P], tag=b_tags[h][pair]) for pair in range(2)]
            product([b_acc[s // 2][:, s % 2, :] for s in range(PACK)], read_q, *g_q[h])
            for pair in range(2):
                planes = slice(2 * pair, 2 * pair + 2)
                nc.vector.tensor_tensor(y[:, planes, cols], b_acc[pair][:], res_raw[:, planes, cols], ALU.add)
                if h == HALVES - 1:
                    nc.sync.dma_start(out=out_rows[:, planes, :], in_=y[:, planes, :])
            y_bf = sbuf("y_bf%d" % h, [P, P, PACK], BF16)
            if h == 0:
                weave(nc.scalar.copy, y_bf[:], y[:, :, cols])
            else:
                weave(nc.vector.tensor_copy, y_bf[:, :80, :], y[:, :, P : P + 80])
                weave(nc.scalar.copy, y_bf[:, 80:, :], y[:, :, P + 80 :])
            nc.vector.quantize_mx(
                out=y_codes[:, cols].bitcast(FP8X4), scales=y_scales[:, cols],
                in_=y_bf[:].rearrange("p q t -> p (q t)"),
            )
            (nc.sync, nc.scalar)[h].dma_start(out=out_words[:, cols], in_=y_codes[:, cols].bitcast(I32))
        for quad in range(4):
            queue = nc.scalar if quad % 2 == 0 else nc.sync
            queue.dma_start(
                out=out_2[0, 4 * quad : 4 * quad + 4, :].bitcast(I32),
                in_=y_scales[32 * quad : 32 * quad + 4, :].bitcast(I32),
            )
